import numpy as np
import ml_dtypes


def mxq(x, axis, fmt="e4m3"):
    dtype, down = {"e4m3": (ml_dtypes.float8_e4m3fn, 7), "e5m2": (ml_dtypes.float8_e5m2, 14)}[fmt]
    v = np.moveaxis(np.asarray(x, np.float32).astype(ml_dtypes.bfloat16).astype(np.float64), axis, -1)
    blocks = v.reshape(v.shape[:-1] + (-1, 32))
    amax = np.abs(blocks).max(-1, keepdims=True)
    byte = np.maximum(np.where(amax > 0, np.frexp(amax)[1] - 1 + 127, 0) - down, 1)
    scale = np.exp2(byte - 127.0)
    codes = (blocks / scale).astype(np.float32).astype(dtype).astype(np.float64)
    return np.moveaxis((codes * scale).reshape(v.shape), -1, axis)


WIDE = False


def mx_kscale(k):
    if not WIDE:
        return np.ones(k)
    levels = np.array([10, -10, 5, -5, 0])
    if k % 512:
        return np.exp2(np.random.permutation(np.resize(levels, k // 32))).repeat(32)
    a = np.empty((k // 512, 16))
    for p in range(k // 512):
        a[p, :8] = np.random.permutation(np.resize(levels, 8))
        for g in range(8):
            far = levels[np.abs(levels - a[p, g]) >= 10]
            a[p, g + 8] = far[np.random.randint(len(far))]
    return np.exp2(a.ravel()).repeat(32)


def f64(x):
    return np.asarray(x).astype(np.float64)


def striped(idx):
    return np.tile(idx.reshape(-1, 16).T, (8, 1)).astype(np.uint16)


def unstriped(offs):
    return offs[:16].T.reshape(-1).astype(np.int64)


def striped8(idx):
    return np.concatenate([x.reshape(-1, 16).T for x in idx]).astype(np.uint16)


def runs(offs, k):
    lists = np.stack([offs[16 * r : 16 * r + 16].T.reshape(-1) for r in range(8)]).astype(np.int64)
    return lists[np.arange(k) % 512 // 64]


def pack_weight(w):
    k, n = w.shape
    w = f64(np.asarray(w, np.float32).astype(ml_dtypes.bfloat16)).reshape(k // 32, 32, n)
    amax = np.abs(w).max(1)
    byte = np.clip(np.where(amax > 0, np.frexp(amax)[1] - 1 + 127 - 7, 1), 1, 254)
    scaled = (w * np.exp2(127.0 - byte)[:, None, :]).reshape(k, n).astype(np.float32)
    words = np.ascontiguousarray(scaled.reshape(k // 512, 128, 4, n).transpose(0, 1, 3, 2)).astype(ml_dtypes.float8_e4m3fn).view(np.uint8)
    return words, np.ascontiguousarray(byte.astype(np.uint8).reshape(k // 512, 16, n))


def unpack_weight(words, scales):
    g, p, n, _ = words.shape
    vals = np.ascontiguousarray(words).view(ml_dtypes.float8_e4m3fn).astype(np.float64) * np.repeat(np.exp2(scales.astype(np.float64) - 127.0), 8, axis=1)[..., None]
    return vals.transpose(0, 1, 3, 2).reshape(g * 512, n)


K, T, S, H, W, G, U = 512, 1024, 256, 512, 128, 2048, 192


def setup_inputs():
    n = np.random.standard_normal
    s = mx_kscale(K)[:, None]
    packed_xT = pack_weight(n((K, T)) * s)
    packed_w1 = pack_weight(n((K, H)) / np.sqrt(2 * K) / s)
    packed_w2 = pack_weight(n((K, H)) / np.sqrt(2 * K) / s)
    packed_dT = pack_weight(n((K, G)) / s)
    perm = np.random.permutation(S)
    return {
        "x_words": packed_xT[0],
        "x_scales": packed_xT[1],
        "w1_words": packed_w1[0],
        "w1_scales": packed_w1[1],
        "w2_words": packed_w2[0],
        "w2_scales": packed_w2[1],
        "gs": (np.random.uniform(0.5, 1.5, (K, 1)) * s).astype(np.float32),
        "d_words": packed_dT[0],
        "d_scales": packed_dT[1],
        "offs": striped8(np.random.randint(0, T, (8, S))),
        "hz": striped8(np.random.randint(0, T, (8, S))),
        "n1": striped(perm[:W]),
        "n2": striped(perm[W:]),
        "n3": striped(np.random.permutation(S)),
        "k1": striped8(np.random.randint(0, G, (8, H))),
        "n4": striped(np.random.permutation(S)[:U]),
        "n5": striped(np.random.permutation(S)[:U]),
    }


def reference(x_words, x_scales, w1_words, w1_scales, w2_words, w2_scales, gs, d_words, d_scales, offs, hz, n1, n2, n3, k1, n4, n5):
    d_k1 = unpack_weight(d_words, d_scales)[np.arange(K)[:, None], runs(k1, K)]
    xq = unpack_weight(x_words, x_scales)[np.arange(K)[:, None], runs(offs, K)]
    x_hz = unpack_weight(x_words, x_scales)[np.arange(K)[:, None], runs(hz, K)]
    y = unpack_weight(w1_words, w1_scales).T @ xq + unpack_weight(w2_words, w2_scales).T @ x_hz
    pa = y[:, unstriped(n1)]
    pb = y[:, unstriped(n2)]
    rb = pa - pb
    ds = np.zeros((H, S))
    ds[:, unstriped(n1)] = pb
    dt = ds.copy()
    dt[:, unstriped(n2)] = rb
    z = f64(gs) * (np.maximum(dt, 0.5 * dt[:, unstriped(n3)]))
    h = 0.0625 * ((d_k1.T @ mxq(z, 0, "e4m3")))
    old = h[:, unstriped(n4)]
    pa2 = h[:, unstriped(n5)]
    ra = old - (0.5 * pa2)
    out = h.copy()
    out[:, unstriped(n4)] = ra
    return out

@@ -1,0 +1,202 @@
+from contextlib import ExitStack
+
+import concourse.mybir as mybir
+
+K, T, S, H, W, G, U = 512, 1024, 256, 512, 128, 2048, 192
+FLOPS = 3 * 2 * K * H * S
+
+F32 = mybir.dt.float32
+BF16 = mybir.dt.bfloat16
+I32 = mybir.dt.int32
+U32 = mybir.dt.uint32
+U16 = mybir.dt.uint16
+U8 = mybir.dt.uint8
+FP8X4 = mybir.dt.float8_e4m3fn_x4
+COPY = mybir.ActivationFunctionType.Copy
+MULT = mybir.AluOpType.mult
+ADD = mybir.AluOpType.add
+SUB = mybir.AluOpType.subtract
+MAX = mybir.AluOpType.max
+
+P = 128
+PACK = 4
+TILES = 4
+HALF = S // 2
+COPIES = 8
+
+
+def words_of(packed):
+    return packed[0].rearrange("p c r -> p (c r)").bitcast(I32)
+
+
+def tile_picked_dhqswapdkdif_none_p_kernel(tc, x_words, x_scales, w1_words, w1_scales, w2_words, w2_scales, gs, d_words, d_scales, offs, hz, n1, n2, n3, k1, n4, n5, out):
+    nc = tc.nc
+    with ExitStack() as ctx:
+        held = ctx.enter_context(tc.tile_pool(name="held", bufs=1))
+        keep = ctx.enter_context(tc.tile_pool(name="keep", bufs=1))
+        psum = ctx.enter_context(tc.psum_pool(name="psum", bufs=8))
+
+        def load_list(name, src):
+            tile = held.tile(list(src.shape), U16, name=name)
+            nc.sync.dma_start(tile[:], src)
+            return tile
+
+        def load_scale_rows(window, scales):
+            rows = scales[0].bitcast(I32)
+            nc.sync.dma_start(out=window[:].bitcast(I32), in_=rows.unsqueeze(1).to_broadcast([16, COPIES, rows.shape[1]]))
+
+        def place_scale_rows(plane, gathered):
+            for i in range(4):
+                nc.sync.dma_start(out=plane[i:P:32, :].bitcast(I32), in_=gathered[COPIES * i : P : 32, :].bitcast(I32))
+
+        xs_win = keep.tile([P, T], U8, name="xs_win", tag="then_d_words", align_bytes=64)
+        l_offs = load_list("l_offs", offs)
+        load_scale_rows(xs_win, x_scales)
+        l_hz = load_list("l_hz", hz)
+        xw_win = keep.tile([P, T], U32, name="xw_win", align_bytes=64)
+        nc.sync.dma_start(out=xw_win[:].bitcast(I32), in_=words_of(x_words))
+        ws_rows = keep.tile([16, 2, H], U8, name="ws_rows", tag="then_d_scales", align_bytes=64)
+        w_raw = []
+        for m, (words, scales) in enumerate(((w1_words, w1_scales), (w2_words, w2_scales))):
+            nc.scalar.dma_start(out=ws_rows[:, m, :].bitcast(I32), in_=scales[0].bitcast(I32))
+            raw = keep.tile([P, H], U32, name=f"w_raw{m}", align_bytes=64)
+            nc.gpsimd.dma_start(out=raw[:].bitcast(I32), in_=words_of(words))
+            w_raw.append(raw)
+        l_n2 = load_list("l_n2", n2)
+        l_n1 = load_list("l_n1", n1)
+        l_n3 = load_list("l_n3", n3)
+        l_k1 = load_list("l_k1", k1)
+        l_n4 = load_list("l_n4", n4)
+        l_n5 = load_list("l_n5", n5)
+
+        ws_plane = keep.tile([P, 2 * H], U8, name="ws_plane", align_bytes=64)
+        x_plane = keep.tile([P, 2 * S], U8, name="x_plane", align_bytes=64)
+        d_plane = keep.tile([P, H], U8, name="d_plane", align_bytes=64)
+        for plane in (ws_plane, x_plane, d_plane):
+            nc.vector.memset(plane[:].bitcast(I32), 0)
+        for q in range(4):
+            nc.sync.dma_start(out=ws_plane[32 * q : 32 * q + 4, :].bitcast(I32), in_=ws_rows[4 * q : 4 * q + 4].rearrange("p m c -> p (m c)").bitcast(I32))
+
+        xs_got = keep.tile([P, 2 * S], U8, name="xs_got", tag="then_gain", align_bytes=64)
+        for m, picks in enumerate((l_offs, l_hz)):
+            nc.vector.tensor_copy(xs_got[:, m * S : (m + 1) * S], xs_win[:].indirect(picks[:]))
+        place_scale_rows(x_plane, xs_got)
+        xw_got = keep.tile([P, 2 * S], U32, name="xw_got", align_bytes=64)
+        for m, picks in enumerate((l_offs, l_hz)):
+            nc.vector.tensor_copy(xw_got[:, m * S : (m + 1) * S], xw_win[:].indirect(picks[:]))
+
+        w_dealt = []
+        for m in range(2):
+            dealt = keep.tile([P, H], U32, name=f"w_dealt{m}", align_bytes=64)
+            nc.scalar.copy(out=dealt[:].rearrange("p (t c) -> p c t", t=PACK), in_=w_raw[m][:].rearrange("p (c t) -> p c t", t=PACK))
+            w_dealt.append(dealt)
+        ws_dealt = []
+        for t in range(TILES):
+            dealt = keep.tile([P, 2, P], U8, name=f"ws_dealt{t}", align_bytes=64)
+            nc.vector.tensor_copy(dealt[:], ws_plane[:].rearrange("p (m c t) -> p t m c", m=2, t=PACK)[:, t])
+            ws_dealt.append(dealt)
+
+        y = []
+        for t in range(TILES):
+            acc = psum.tile([P, S], F32, name=f"y_acc{t}", tag="acc")
+            for m in range(2):
+                nc.tensor.matmul_mx(
+                    out=acc[:],
+                    lhsT=w_dealt[m][:, t * P : (t + 1) * P].bitcast(FP8X4),
+                    lhsT_scale=ws_dealt[t][:, m, :],
+                    rhs=xw_got[:, m * S : (m + 1) * S].bitcast(FP8X4),
+                    rhs_scale=x_plane[:, m * S : (m + 1) * S],
+                    start=(m == 0),
+                    stop=(m == 1),
+                )
+            rows = keep.tile([P, S], F32, name=f"y{t}")
+            if t == 0:
+                nc.scalar.activation(rows[:], acc[:], COPY)
+            else:
+                nc.vector.tensor_copy(rows[:], acc[:])
+            y.append(rows)
+
+        dw_win = keep.tile([P, G], U32, name="dw_win", tag="then_d_words", align_bytes=64)
+        nc.sync.dma_start(out=dw_win[:].bitcast(I32), in_=words_of(d_words))
+        ds_win = keep.tile([P, G], U8, name="ds_win", tag="then_d_scales", align_bytes=64)
+        load_scale_rows(ds_win, d_scales)
+        gain = keep.tile([P, PACK], F32, name="gain", tag="then_gain", align_bytes=64)
+        nc.sync.dma_start(out=gain[:], in_=gs.rearrange("(p t) o -> p (t o)", t=PACK))
+        ds_got = keep.tile([P, H], U8, name="ds_got", align_bytes=64)
+        dw_got = keep.tile([P, H], U32, name="dw_got", align_bytes=64)
+
+        def gather_codes(got, window, piece):
+            nc.vector.tensor_copy(got[:, piece * 256 : (piece + 1) * 256], window[:].indirect(l_k1[:, piece * 16 : (piece + 1) * 16]))
+
+        z_bf = [keep.tile([P, HALF, PACK], BF16, name=f"z_bf{a}", align_bytes=64) for a in range(2)]
+        dt = [keep.tile([P, S], F32, name=f"dt{t}") for t in range(TILES)]
+
+        def weigh(t, a):
+            cols = slice(a * HALF, (a + 1) * HALF)
+            far = keep.tile([P, HALF], F32, name=f"far{t}_{a}")
+            nc.scalar.activation(far[:], dt[t][:].indirect(l_n3[:, a * HALF // 16 : (a + 1) * HALF // 16]), COPY)
+            top = keep.tile([P, HALF], F32, name=f"top{t}_{a}")
+            nc.vector.scalar_tensor_tensor(top[:], far[:], 0.5, dt[t][:, cols], MULT, MAX)
+            nc.vector.tensor_scalar(z_bf[a][:, :, t], top[:], gain[:, t : t + 1], None, MULT)
+
+        for t in range(TILES):
+            pa = keep.tile([P, W], F32, name=f"pa{t}")
+            pb = keep.tile([P, W], F32, name=f"pb{t}")
+            rb = keep.tile([P, W], F32, name=f"rb{t}")
+            nc.scalar.activation(pb[:], y[t][:].indirect(l_n2[:]), COPY)
+            nc.scalar.activation(pa[:], y[t][:].indirect(l_n1[:]), COPY)
+            nc.vector.tensor_tensor(rb[:], pa[:], pb[:], SUB)
+            nc.scalar.activation(dt[t][:].indirect(l_n1[:]), pb[:], COPY)
+            if t > 0:
+                weigh(t - 1, 0)
+            nc.scalar.activation(dt[t][:].indirect(l_n2[:]), rb[:], COPY)
+            if t > 0:
+                weigh(t - 1, 1)
+            if t == 0:
+                for piece in range(2):
+                    gather_codes(ds_got, ds_win, piece)
+                place_scale_rows(d_plane, ds_got)
+            if t == 1:
+                for piece in range(2):
+                    gather_codes(dw_got, dw_win, piece)
+
+        h = [keep.tile([P, S], F32, name=f"h{t}") for t in range(TILES)]
+        h_acc = [None] + [psum.tile([P, S], F32, name=f"h_acc{t}", tag="acc") for t in range(1, TILES)]
+        for a in range(2):
+            cols = slice(a * HALF, (a + 1) * HALF)
+            weigh(TILES - 1, a)
+            z_words = keep.tile([P, HALF], U32, name=f"z_words{a}", align_bytes=64)
+            z_plane = keep.tile([P, HALF], U8, name=f"z_plane{a}", align_bytes=64)
+            nc.vector.quantize_mx(out=z_words[:].bitcast(FP8X4), scales=z_plane[:], in_=z_bf[a][:].rearrange("p c t -> p (c t)"))
+            first = psum.tile([P, HALF], F32, name=f"h_first{a}", tag="acc")
+            for t in range(TILES):
+                nc.tensor.matmul_mx(
+                    out=first[:] if t == 0 else h_acc[t][:, cols],
+                    lhsT=dw_got[:, t * P : (t + 1) * P].bitcast(FP8X4),
+                    lhsT_scale=d_plane[:, t * P : (t + 1) * P],
+                    rhs=z_words[:].bitcast(FP8X4),
+                    rhs_scale=z_plane[:],
+                    start=True,
+                    stop=True,
+                )
+            nc.scalar.activation(h[0][:, cols], first[:], COPY, scale=0.0625)
+        for t in range(1, TILES):
+            nc.vector.tensor_scalar(h[t][:], h_acc[t][:], 0.0625, None, MULT)
+
+        ra = []
+
+        def put_back(t):
+            nc.scalar.activation(h[t][:].indirect(l_n4[:]), ra[t][:], COPY)
+            nc.sync.dma_start(out=out[t * P : (t + 1) * P, :], in_=h[t][:])
+
+        for t in range(TILES):
+            old = keep.tile([P, U], F32, name=f"old{t}")
+            pa2 = keep.tile([P, U], F32, name=f"pa2_{t}")
+            new = keep.tile([P, U], F32, name=f"ra{t}")
+            nc.scalar.activation(old[:], h[t][:].indirect(l_n4[:]), COPY)
+            nc.scalar.activation(pa2[:], h[t][:].indirect(l_n5[:]), COPY)
+            nc.vector.scalar_tensor_tensor(new[:], pa2[:], -0.5, old[:], MULT, ADD)
+            ra.append(new)
+            if t > 0:
+                put_back(t - 1)
+        put_back(TILES - 1)

@@ -22,6 +22,7 @@ P = 128
 PACK = 4
 TILES = 4
 HALF = S // 2
+SPARE = 16
 COPIES = 8
 
 
@@ -41,33 +42,28 @@ def tile_picked_dhqswapdkdif_none_p_kernel(tc, x_words, x_scales, w1_words, w1_s
             nc.sync.dma_start(tile[:], src)
             return tile
 
-        def load_scale_rows(window, scales):
+        def load_scale_rows(queue, window, scales):
             rows = scales[0].bitcast(I32)
-            nc.sync.dma_start(out=window[:].bitcast(I32), in_=rows.unsqueeze(1).to_broadcast([16, COPIES, rows.shape[1]]))
+            queue.dma_start(out=window[:].bitcast(I32), in_=rows.unsqueeze(1).to_broadcast([16, COPIES, rows.shape[1]]))
 
         def place_scale_rows(plane, gathered):
             for i in range(4):
                 nc.sync.dma_start(out=plane[i:P:32, :].bitcast(I32), in_=gathered[COPIES * i : P : 32, :].bitcast(I32))
 
-        xs_win = keep.tile([P, T], U8, name="xs_win", tag="then_d_words", align_bytes=64)
+        xs_win = keep.tile([P, T], U8, name="xs_win", tag="then_d_scales", align_bytes=64)
         l_offs = load_list("l_offs", offs)
-        load_scale_rows(xs_win, x_scales)
+        load_scale_rows(nc.sync, xs_win, x_scales)
         l_hz = load_list("l_hz", hz)
-        xw_win = keep.tile([P, T], U32, name="xw_win", align_bytes=64)
+        xw_win = keep.tile([P, T], U32, name="xw_win", tag="then_d_words", align_bytes=64)
         nc.sync.dma_start(out=xw_win[:].bitcast(I32), in_=words_of(x_words))
-        ws_rows = keep.tile([16, 2, H], U8, name="ws_rows", tag="then_d_scales", align_bytes=64)
+        ws_rows = keep.tile([16, 2, H], U8, name="ws_rows", align_bytes=64)
         w_raw = []
         for m, (words, scales) in enumerate(((w1_words, w1_scales), (w2_words, w2_scales))):
             nc.scalar.dma_start(out=ws_rows[:, m, :].bitcast(I32), in_=scales[0].bitcast(I32))
             raw = keep.tile([P, H], U32, name=f"w_raw{m}", align_bytes=64)
-            nc.gpsimd.dma_start(out=raw[:].bitcast(I32), in_=words_of(words))
             w_raw.append(raw)
-        l_n2 = load_list("l_n2", n2)
-        l_n1 = load_list("l_n1", n1)
-        l_n3 = load_list("l_n3", n3)
-        l_k1 = load_list("l_k1", k1)
-        l_n4 = load_list("l_n4", n4)
-        l_n5 = load_list("l_n5", n5)
+        nc.gpsimd.dma_start(out=w_raw[0][:].bitcast(I32), in_=words_of(w1_words))
+        nc.gpsimd.dma_start(out=w_raw[1][:].bitcast(I32), in_=words_of(w2_words))
 
         ws_plane = keep.tile([P, 2 * H], U8, name="ws_plane", align_bytes=64)
         x_plane = keep.tile([P, 2 * S], U8, name="x_plane", align_bytes=64)
@@ -77,10 +73,12 @@ def tile_picked_dhqswapdkdif_none_p_kernel(tc, x_words, x_scales, w1_words, w1_s
         for q in range(4):
             nc.sync.dma_start(out=ws_plane[32 * q : 32 * q + 4, :].bitcast(I32), in_=ws_rows[4 * q : 4 * q + 4].rearrange("p m c -> p (m c)").bitcast(I32))
 
-        xs_got = keep.tile([P, 2 * S], U8, name="xs_got", tag="then_gain", align_bytes=64)
+        xs_got = keep.tile([P, 2 * S], U8, name="xs_got", align_bytes=64)
         for m, picks in enumerate((l_offs, l_hz)):
             nc.vector.tensor_copy(xs_got[:, m * S : (m + 1) * S], xs_win[:].indirect(picks[:]))
         place_scale_rows(x_plane, xs_got)
+        l_n2 = load_list("l_n2", n2)
+        l_n1 = load_list("l_n1", n1)
         xw_got = keep.tile([P, 2 * S], U32, name="xw_got", align_bytes=64)
         for m, picks in enumerate((l_offs, l_hz)):
             nc.vector.tensor_copy(xw_got[:, m * S : (m + 1) * S], xw_win[:].indirect(picks[:]))
@@ -116,58 +114,74 @@ def tile_picked_dhqswapdkdif_none_p_kernel(tc, x_words, x_scales, w1_words, w1_s
                 nc.vector.tensor_copy(rows[:], acc[:])
             y.append(rows)
 
+        ds_win = keep.tile([P, G], U8, name="ds_win", tag="then_d_scales", align_bytes=64)
+        load_scale_rows(nc.gpsimd, ds_win, d_scales)
         dw_win = keep.tile([P, G], U32, name="dw_win", tag="then_d_words", align_bytes=64)
         nc.sync.dma_start(out=dw_win[:].bitcast(I32), in_=words_of(d_words))
-        ds_win = keep.tile([P, G], U8, name="ds_win", tag="then_d_scales", align_bytes=64)
-        load_scale_rows(ds_win, d_scales)
-        gain = keep.tile([P, PACK], F32, name="gain", tag="then_gain", align_bytes=64)
-        nc.sync.dma_start(out=gain[:], in_=gs.rearrange("(p t) o -> p (t o)", t=PACK))
+        l_k1 = load_list("l_k1", k1)
+        l_n3 = load_list("l_n3", n3)
+        l_n4 = load_list("l_n4", n4)
+        l_n5 = load_list("l_n5", n5)
+        gain = keep.tile([P, PACK], F32, name="gain")
+        nc.gpsimd.dma_start(out=gain[:], in_=gs.rearrange("(p t) o -> p (t o)", t=PACK))
         ds_got = keep.tile([P, H], U8, name="ds_got", align_bytes=64)
         dw_got = keep.tile([P, H], U32, name="dw_got", align_bytes=64)
 
         def gather_codes(got, window, piece):
             nc.vector.tensor_copy(got[:, piece * 256 : (piece + 1) * 256], window[:].indirect(l_k1[:, piece * 16 : (piece + 1) * 16]))
 
-        z_bf = [keep.tile([P, HALF, PACK], BF16, name=f"z_bf{a}", align_bytes=64) for a in range(2)]
-        dt = [keep.tile([P, S], F32, name=f"dt{t}") for t in range(TILES)]
+        z_bf = keep.tile([P, S, PACK], BF16, name="z_bf", align_bytes=64)
+        dt = [keep.tile([P, S + SPARE], F32, name=f"dt{t}") for t in range(TILES)]
+        for t in range(TILES):
+            nc.vector.memset(dt[t][:, S:], 0.0)
 
-        def weigh(t, a):
-            cols = slice(a * HALF, (a + 1) * HALF)
-            far = keep.tile([P, HALF], F32, name=f"far{t}_{a}")
-            nc.scalar.activation(far[:], dt[t][:].indirect(l_n3[:, a * HALF // 16 : (a + 1) * HALF // 16]), COPY)
-            top = keep.tile([P, HALF], F32, name=f"top{t}_{a}")
-            nc.vector.scalar_tensor_tensor(top[:], far[:], 0.5, dt[t][:, cols], MULT, MAX)
-            nc.vector.tensor_scalar(z_bf[a][:, :, t], top[:], gain[:, t : t + 1], None, MULT)
+        def larger(t, c0, c1):
+            far = keep.tile([P, c1 - c0], F32, name=f"far{t}_{c0}")
+            nc.scalar.activation(far[:], dt[t][:].indirect(l_n3[:, c0 // 16 : c1 // 16]), COPY)
+            top = keep.tile([P, c1 - c0], F32, name=f"top{t}_{c0}", tag="then_d_words" if t == 0 else f"top{t}_{c0}", align_bytes=64)
+            nc.vector.scalar_tensor_tensor(top[:], far[:], 0.5, dt[t][:, c0:c1], MULT, MAX)
+            return top
 
+        def weigh(t, c0, c1, top):
+            nc.vector.tensor_scalar(z_bf[:, c0:c1, t], top[:], gain[:, t : t + 1], None, MULT)
+
+        rb = []
         for t in range(TILES):
             pa = keep.tile([P, W], F32, name=f"pa{t}")
             pb = keep.tile([P, W], F32, name=f"pb{t}")
-            rb = keep.tile([P, W], F32, name=f"rb{t}")
             nc.scalar.activation(pb[:], y[t][:].indirect(l_n2[:]), COPY)
             nc.scalar.activation(pa[:], y[t][:].indirect(l_n1[:]), COPY)
-            nc.vector.tensor_tensor(rb[:], pa[:], pb[:], SUB)
-            nc.scalar.activation(dt[t][:].indirect(l_n1[:]), pb[:], COPY)
-            if t > 0:
-                weigh(t - 1, 0)
-            nc.scalar.activation(dt[t][:].indirect(l_n2[:]), rb[:], COPY)
-            if t > 0:
-                weigh(t - 1, 1)
-            if t == 0:
+            if t == TILES - 1:
                 for piece in range(2):
                     gather_codes(ds_got, ds_win, piece)
                 place_scale_rows(d_plane, ds_got)
-            if t == 1:
-                for piece in range(2):
-                    gather_codes(dw_got, dw_win, piece)
+            diff = keep.tile([P, W], F32, name=f"rb{t}", tag="then_d_scales" if t == TILES - 1 else f"rb{t}", align_bytes=64)
+            nc.vector.tensor_tensor(diff[:], pa[:], pb[:], SUB)
+            rb.append(diff)
+            nc.scalar.activation(dt[t][:].indirect(l_n1[:]), pb[:], COPY)
+        for piece in range(2):
+            gather_codes(dw_got, dw_win, piece)
+
+        def put_differences(t):
+            nc.scalar.activation(dt[t][:].indirect(l_n2[:]), rb[t][:], COPY)
+
+        put_differences(0)
+        for t in range(TILES - 1):
+            if t + 1 < TILES - 1:
+                put_differences(t + 1)
+            weigh(t, 0, S, larger(t, 0, S))
+        put_differences(TILES - 1)
 
         h = [keep.tile([P, S], F32, name=f"h{t}") for t in range(TILES)]
         h_acc = [None] + [psum.tile([P, S], F32, name=f"h_acc{t}", tag="acc") for t in range(1, TILES)]
+        tops = [larger(TILES - 1, a * HALF, (a + 1) * HALF) for a in range(2)]
+        for a in range(2):
+            weigh(TILES - 1, a * HALF, (a + 1) * HALF, tops[a])
         for a in range(2):
             cols = slice(a * HALF, (a + 1) * HALF)
-            weigh(TILES - 1, a)
             z_words = keep.tile([P, HALF], U32, name=f"z_words{a}", align_bytes=64)
             z_plane = keep.tile([P, HALF], U8, name=f"z_plane{a}", align_bytes=64)
-            nc.vector.quantize_mx(out=z_words[:].bitcast(FP8X4), scales=z_plane[:], in_=z_bf[a][:].rearrange("p c t -> p (c t)"))
+            nc.vector.quantize_mx(out=z_words[:].bitcast(FP8X4), scales=z_plane[:], in_=z_bf[:, cols, :].rearrange("p c t -> p (c t)"))
             first = psum.tile([P, HALF], F32, name=f"h_first{a}", tag="acc")
             for t in range(TILES):
                 nc.tensor.matmul_mx(

@@ -50,11 +50,11 @@ def tile_picked_dhqswapdkdif_none_p_kernel(tc, x_words, x_scales, w1_words, w1_s
             for i in range(4):
                 nc.sync.dma_start(out=plane[i:P:32, :].bitcast(I32), in_=gathered[COPIES * i : P : 32, :].bitcast(I32))
 
-        xs_win = keep.tile([P, T], U8, name="xs_win", tag="then_d_scales", align_bytes=64)
+        xs_win = keep.tile([P, T], U8, name="xs_win", align_bytes=64)
         l_offs = load_list("l_offs", offs)
         load_scale_rows(nc.sync, xs_win, x_scales)
         l_hz = load_list("l_hz", hz)
-        xw_win = keep.tile([P, T], U32, name="xw_win", tag="then_d_words", align_bytes=64)
+        xw_win = keep.tile([P, T], U32, name="xw_win", align_bytes=64)
         nc.sync.dma_start(out=xw_win[:].bitcast(I32), in_=words_of(x_words))
         ws_rows = keep.tile([16, 2, H], U8, name="ws_rows", align_bytes=64)
         w_raw = []
@@ -65,6 +65,8 @@ def tile_picked_dhqswapdkdif_none_p_kernel(tc, x_words, x_scales, w1_words, w1_s
         nc.gpsimd.dma_start(out=w_raw[0][:].bitcast(I32), in_=words_of(w1_words))
         nc.gpsimd.dma_start(out=w_raw[1][:].bitcast(I32), in_=words_of(w2_words))
 
+        l_n2 = load_list("l_n2", n2)
+        l_n1 = load_list("l_n1", n1)
         ws_plane = keep.tile([P, 2 * H], U8, name="ws_plane", align_bytes=64)
         x_plane = keep.tile([P, 2 * S], U8, name="x_plane", align_bytes=64)
         d_plane = keep.tile([P, H], U8, name="d_plane", align_bytes=64)
@@ -73,13 +75,11 @@ def tile_picked_dhqswapdkdif_none_p_kernel(tc, x_words, x_scales, w1_words, w1_s
         for q in range(4):
             nc.sync.dma_start(out=ws_plane[32 * q : 32 * q + 4, :].bitcast(I32), in_=ws_rows[4 * q : 4 * q + 4].rearrange("p m c -> p (m c)").bitcast(I32))
 
-        xs_got = keep.tile([P, 2 * S], U8, name="xs_got", align_bytes=64)
+        xs_got = keep.tile([P, 2 * S], U8, name="xs_got", tag="then_d_scales", align_bytes=64)
         for m, picks in enumerate((l_offs, l_hz)):
             nc.vector.tensor_copy(xs_got[:, m * S : (m + 1) * S], xs_win[:].indirect(picks[:]))
         place_scale_rows(x_plane, xs_got)
-        l_n2 = load_list("l_n2", n2)
-        l_n1 = load_list("l_n1", n1)
-        xw_got = keep.tile([P, 2 * S], U32, name="xw_got", align_bytes=64)
+        xw_got = keep.tile([P, 2 * S], U32, name="xw_got", tag="then_d_words", align_bytes=64)
         for m, picks in enumerate((l_offs, l_hz)):
             nc.vector.tensor_copy(xw_got[:, m * S : (m + 1) * S], xw_win[:].indirect(picks[:]))
 
@@ -94,28 +94,28 @@ def tile_picked_dhqswapdkdif_none_p_kernel(tc, x_words, x_scales, w1_words, w1_s
             nc.vector.tensor_copy(dealt[:], ws_plane[:].rearrange("p (m c t) -> p t m c", m=2, t=PACK)[:, t])
             ws_dealt.append(dealt)
 
-        y = []
-        for t in range(TILES):
-            acc = psum.tile([P, S], F32, name=f"y_acc{t}", tag="acc")
-            for m in range(2):
+        def project(t, c0, c1):
+            acc = psum.tile([P, c1 - c0], F32, name=f"y_acc{t}_{c0}", tag="acc")
+            for m in (1, 0):
                 nc.tensor.matmul_mx(
                     out=acc[:],
                     lhsT=w_dealt[m][:, t * P : (t + 1) * P].bitcast(FP8X4),
                     lhsT_scale=ws_dealt[t][:, m, :],
-                    rhs=xw_got[:, m * S : (m + 1) * S].bitcast(FP8X4),
-                    rhs_scale=x_plane[:, m * S : (m + 1) * S],
-                    start=(m == 0),
-                    stop=(m == 1),
+                    rhs=xw_got[:, m * S + c0 : m * S + c1].bitcast(FP8X4),
+                    rhs_scale=x_plane[:, m * S + c0 : m * S + c1],
+                    start=(m == 1),
+                    stop=(m == 0),
                 )
-            rows = keep.tile([P, S], F32, name=f"y{t}")
-            if t == 0:
-                nc.scalar.activation(rows[:], acc[:], COPY)
-            else:
-                nc.vector.tensor_copy(rows[:], acc[:])
-            y.append(rows)
+            return acc
+
+        y = [keep.tile([P, S], F32, name=f"y{t}") for t in range(TILES)]
+        nc.vector.tensor_copy(y[0][:, :HALF], project(0, 0, HALF)[:])
+        nc.scalar.activation(y[0][:, HALF:], project(0, HALF, S)[:], COPY)
+        for t in range(1, TILES):
+            nc.vector.tensor_copy(y[t][:], project(t, 0, S)[:])
 
         ds_win = keep.tile([P, G], U8, name="ds_win", tag="then_d_scales", align_bytes=64)
-        load_scale_rows(nc.gpsimd, ds_win, d_scales)
+        load_scale_rows(nc.sync, ds_win, d_scales)
         dw_win = keep.tile([P, G], U32, name="dw_win", tag="then_d_words", align_bytes=64)
         nc.sync.dma_start(out=dw_win[:].bitcast(I32), in_=words_of(d_words))
         l_k1 = load_list("l_k1", k1)
@@ -135,16 +135,6 @@ def tile_picked_dhqswapdkdif_none_p_kernel(tc, x_words, x_scales, w1_words, w1_s
         for t in range(TILES):
             nc.vector.memset(dt[t][:, S:], 0.0)
 
-        def larger(t, c0, c1):
-            far = keep.tile([P, c1 - c0], F32, name=f"far{t}_{c0}")
-            nc.scalar.activation(far[:], dt[t][:].indirect(l_n3[:, c0 // 16 : c1 // 16]), COPY)
-            top = keep.tile([P, c1 - c0], F32, name=f"top{t}_{c0}", tag="then_d_words" if t == 0 else f"top{t}_{c0}", align_bytes=64)
-            nc.vector.scalar_tensor_tensor(top[:], far[:], 0.5, dt[t][:, c0:c1], MULT, MAX)
-            return top
-
-        def weigh(t, c0, c1, top):
-            nc.vector.tensor_scalar(z_bf[:, c0:c1, t], top[:], gain[:, t : t + 1], None, MULT)
-
         rb = []
         for t in range(TILES):
             pa = keep.tile([P, W], F32, name=f"pa{t}")
@@ -162,6 +152,16 @@ def tile_picked_dhqswapdkdif_none_p_kernel(tc, x_words, x_scales, w1_words, w1_s
         for piece in range(2):
             gather_codes(dw_got, dw_win, piece)
 
+        top = keep.tile([P, TILES, S], F32, name="top", tag="then_d_words", align_bytes=64)
+
+        def larger(t, c0, c1):
+            far = keep.tile([P, c1 - c0], F32, name=f"far{t}_{c0}")
+            nc.scalar.activation(far[:], dt[t][:].indirect(l_n3[:, c0 // 16 : c1 // 16]), COPY)
+            nc.vector.scalar_tensor_tensor(top[:, t, c0:c1], far[:], 0.5, dt[t][:, c0:c1], MULT, MAX)
+
+        def weigh(t, c0, c1):
+            nc.vector.tensor_scalar(z_bf[:, c0:c1, t], top[:, t, c0:c1], gain[:, t : t + 1], None, MULT)
+
         def put_differences(t):
             nc.scalar.activation(dt[t][:].indirect(l_n2[:]), rb[t][:], COPY)
 
@@ -169,14 +169,16 @@ def tile_picked_dhqswapdkdif_none_p_kernel(tc, x_words, x_scales, w1_words, w1_s
         for t in range(TILES - 1):
             if t + 1 < TILES - 1:
                 put_differences(t + 1)
-            weigh(t, 0, S, larger(t, 0, S))
+            larger(t, 0, S)
+            weigh(t, 0, S)
         put_differences(TILES - 1)
 
         h = [keep.tile([P, S], F32, name=f"h{t}") for t in range(TILES)]
         h_acc = [None] + [psum.tile([P, S], F32, name=f"h_acc{t}", tag="acc") for t in range(1, TILES)]
-        tops = [larger(TILES - 1, a * HALF, (a + 1) * HALF) for a in range(2)]
         for a in range(2):
-            weigh(TILES - 1, a * HALF, (a + 1) * HALF, tops[a])
+            larger(TILES - 1, a * HALF, (a + 1) * HALF)
+        for a in range(2):
+            weigh(TILES - 1, a * HALF, (a + 1) * HALF)
         for a in range(2):
             cols = slice(a * HALF, (a + 1) * HALF)
             z_words = keep.tile([P, HALF], U32, name=f"z_words{a}", align_bytes=64)

@@ -46,9 +46,9 @@ def tile_picked_dhqswapdkdif_none_p_kernel(tc, x_words, x_scales, w1_words, w1_s
             rows = scales[0].bitcast(I32)
             queue.dma_start(out=window[:].bitcast(I32), in_=rows.unsqueeze(1).to_broadcast([16, COPIES, rows.shape[1]]))
 
-        def place_scale_rows(plane, gathered):
+        def place_scale_rows(queues, plane, gathered):
             for i in range(4):
-                nc.sync.dma_start(out=plane[i:P:32, :].bitcast(I32), in_=gathered[COPIES * i : P : 32, :].bitcast(I32))
+                queues[i % len(queues)].dma_start(out=plane[i:P:32, :].bitcast(I32), in_=gathered[COPIES * i : P : 32, :].bitcast(I32))
 
         xs_win = keep.tile([P, T], U8, name="xs_win", align_bytes=64)
         l_offs = load_list("l_offs", offs)
@@ -78,7 +78,7 @@ def tile_picked_dhqswapdkdif_none_p_kernel(tc, x_words, x_scales, w1_words, w1_s
         xs_got = keep.tile([P, 2 * S], U8, name="xs_got", tag="then_d_scales", align_bytes=64)
         for m, picks in enumerate((l_offs, l_hz)):
             nc.vector.tensor_copy(xs_got[:, m * S : (m + 1) * S], xs_win[:].indirect(picks[:]))
-        place_scale_rows(x_plane, xs_got)
+        place_scale_rows((nc.sync,), x_plane, xs_got)
         xw_got = keep.tile([P, 2 * S], U32, name="xw_got", tag="then_d_words", align_bytes=64)
         for m, picks in enumerate((l_offs, l_hz)):
             nc.vector.tensor_copy(xw_got[:, m * S : (m + 1) * S], xw_win[:].indirect(picks[:]))
@@ -144,7 +144,7 @@ def tile_picked_dhqswapdkdif_none_p_kernel(tc, x_words, x_scales, w1_words, w1_s
             if t == TILES - 1:
                 for piece in range(2):
                     gather_codes(ds_got, ds_win, piece)
-                place_scale_rows(d_plane, ds_got)
+                place_scale_rows((nc.sync,), d_plane, ds_got)
             diff = keep.tile([P, W], F32, name=f"rb{t}", tag="then_d_scales" if t == TILES - 1 else f"rb{t}", align_bytes=64)
             nc.vector.tensor_tensor(diff[:], pa[:], pb[:], SUB)
             rb.append(diff)
@@ -173,31 +173,34 @@ def tile_picked_dhqswapdkdif_none_p_kernel(tc, x_words, x_scales, w1_words, w1_s
             weigh(t, 0, S)
         put_differences(TILES - 1)
 
+        z_words = keep.tile([P, S], U32, name="z_words", align_bytes=64)
+        z_plane = keep.tile([P, S], U8, name="z_plane", align_bytes=64)
+        halves = [(a * HALF, (a + 1) * HALF) for a in range(2)]
+        for c0, c1 in halves:
+            larger(TILES - 1, c0, c1)
+        for c0, c1 in halves:
+            weigh(TILES - 1, c0, c1)
+        for c0, c1 in halves:
+            nc.vector.quantize_mx(out=z_words[:, c0:c1].bitcast(FP8X4), scales=z_plane[:, c0:c1], in_=z_bf[:, c0:c1, :].rearrange("p c t -> p (c t)"))
+
+        def decode(t, c0, c1):
+            acc = psum.tile([P, c1 - c0], F32, name=f"h_acc{t}_{c0}", tag="acc")
+            nc.tensor.matmul_mx(
+                out=acc[:],
+                lhsT=dw_got[:, t * P : (t + 1) * P].bitcast(FP8X4),
+                lhsT_scale=d_plane[:, t * P : (t + 1) * P],
+                rhs=z_words[:, c0:c1].bitcast(FP8X4),
+                rhs_scale=z_plane[:, c0:c1],
+                start=True,
+                stop=True,
+            )
+            return acc
+
         h = [keep.tile([P, S], F32, name=f"h{t}") for t in range(TILES)]
-        h_acc = [None] + [psum.tile([P, S], F32, name=f"h_acc{t}", tag="acc") for t in range(1, TILES)]
-        for a in range(2):
-            larger(TILES - 1, a * HALF, (a + 1) * HALF)
-        for a in range(2):
-            weigh(TILES - 1, a * HALF, (a + 1) * HALF)
-        for a in range(2):
-            cols = slice(a * HALF, (a + 1) * HALF)
-            z_words = keep.tile([P, HALF], U32, name=f"z_words{a}", align_bytes=64)
-            z_plane = keep.tile([P, HALF], U8, name=f"z_plane{a}", align_bytes=64)
-            nc.vector.quantize_mx(out=z_words[:].bitcast(FP8X4), scales=z_plane[:], in_=z_bf[:, cols, :].rearrange("p c t -> p (c t)"))
-            first = psum.tile([P, HALF], F32, name=f"h_first{a}", tag="acc")
-            for t in range(TILES):
-                nc.tensor.matmul_mx(
-                    out=first[:] if t == 0 else h_acc[t][:, cols],
-                    lhsT=dw_got[:, t * P : (t + 1) * P].bitcast(FP8X4),
-                    lhsT_scale=d_plane[:, t * P : (t + 1) * P],
-                    rhs=z_words[:].bitcast(FP8X4),
-                    rhs_scale=z_plane[:],
-                    start=True,
-                    stop=True,
-                )
-            nc.scalar.activation(h[0][:, cols], first[:], COPY, scale=0.0625)
+        for c0, c1 in halves:
+            nc.scalar.activation(h[0][:, c0:c1], decode(0, c0, c1)[:], COPY, scale=0.0625)
         for t in range(1, TILES):
-            nc.vector.tensor_scalar(h[t][:], h_acc[t][:], 0.0625, None, MULT)
+            nc.vector.tensor_scalar(h[t][:], decode(t, 0, S)[:], 0.0625, None, MULT)
 
         ra = []
 

from contextlib import ExitStack

import concourse.mybir as mybir

K, T, S, H, W, G, U = 512, 1024, 256, 512, 128, 2048, 192
FLOPS = 3 * 2 * K * H * S

F32 = mybir.dt.float32
BF16 = mybir.dt.bfloat16
I32 = mybir.dt.int32
U32 = mybir.dt.uint32
U16 = mybir.dt.uint16
U8 = mybir.dt.uint8
FP8X4 = mybir.dt.float8_e4m3fn_x4
COPY = mybir.ActivationFunctionType.Copy
MULT = mybir.AluOpType.mult
ADD = mybir.AluOpType.add
SUB = mybir.AluOpType.subtract
MAX = mybir.AluOpType.max

P = 128
PACK = 4
TILES = 4
HALF = S // 2
SPARE = 16
COPIES = 8


def words_of(packed):
    return packed[0].rearrange("p c r -> p (c r)").bitcast(I32)


def tile_picked_dhqswapdkdif_none_p_kernel(tc, x_words, x_scales, w1_words, w1_scales, w2_words, w2_scales, gs, d_words, d_scales, offs, hz, n1, n2, n3, k1, n4, n5, out):
    nc = tc.nc
    with ExitStack() as ctx:
        held = ctx.enter_context(tc.tile_pool(name="held", bufs=1))
        keep = ctx.enter_context(tc.tile_pool(name="keep", bufs=1))
        psum = ctx.enter_context(tc.psum_pool(name="psum", bufs=8))

        def load_list(name, src):
            tile = held.tile(list(src.shape), U16, name=name)
            nc.sync.dma_start(tile[:], src)
            return tile

        def load_scale_rows(queue, window, scales):
            rows = scales[0].bitcast(I32)
            queue.dma_start(out=window[:].bitcast(I32), in_=rows.unsqueeze(1).to_broadcast([16, COPIES, rows.shape[1]]))

        def place_scale_rows(queues, plane, gathered):
            for i in range(4):
                queues[i % len(queues)].dma_start(out=plane[i:P:32, :].bitcast(I32), in_=gathered[COPIES * i : P : 32, :].bitcast(I32))

        xs_win = keep.tile([P, T], U8, name="xs_win", align_bytes=64)
        l_offs = load_list("l_offs", offs)
        load_scale_rows(nc.sync, xs_win, x_scales)
        l_hz = load_list("l_hz", hz)
        xw_win = keep.tile([P, T], U32, name="xw_win", align_bytes=64)
        nc.sync.dma_start(out=xw_win[:].bitcast(I32), in_=words_of(x_words))
        ws_rows = keep.tile([16, 2, H], U8, name="ws_rows", align_bytes=64)
        w_raw = []
        for m, (words, scales) in enumerate(((w1_words, w1_scales), (w2_words, w2_scales))):
            nc.scalar.dma_start(out=ws_rows[:, m, :].bitcast(I32), in_=scales[0].bitcast(I32))
            raw = keep.tile([P, H], U32, name=f"w_raw{m}", align_bytes=64)
            w_raw.append(raw)
        nc.gpsimd.dma_start(out=w_raw[0][:].bitcast(I32), in_=words_of(w1_words))
        nc.gpsimd.dma_start(out=w_raw[1][:].bitcast(I32), in_=words_of(w2_words))

        l_n2 = load_list("l_n2", n2)
        l_n1 = load_list("l_n1", n1)
        ws_plane = keep.tile([P, 2 * H], U8, name="ws_plane", align_bytes=64)
        x_plane = keep.tile([P, 2 * S], U8, name="x_plane", align_bytes=64)
        d_plane = keep.tile([P, H], U8, name="d_plane", align_bytes=64)
        for plane in (ws_plane, x_plane, d_plane):
            nc.vector.memset(plane[:].bitcast(I32), 0)
        for q in range(4):
            nc.sync.dma_start(out=ws_plane[32 * q : 32 * q + 4, :].bitcast(I32), in_=ws_rows[4 * q : 4 * q + 4].rearrange("p m c -> p (m c)").bitcast(I32))

        xs_got = keep.tile([P, 2 * S], U8, name="xs_got", tag="then_d_scales", align_bytes=64)
        for m, picks in enumerate((l_offs, l_hz)):
            nc.vector.tensor_copy(xs_got[:, m * S : (m + 1) * S], xs_win[:].indirect(picks[:]))
        place_scale_rows((nc.sync,), x_plane, xs_got)
        xw_got = keep.tile([P, 2 * S], U32, name="xw_got", tag="then_d_words", align_bytes=64)
        for m, picks in enumerate((l_offs, l_hz)):
            nc.vector.tensor_copy(xw_got[:, m * S : (m + 1) * S], xw_win[:].indirect(picks[:]))

        w_dealt = []
        for m in range(2):
            dealt = keep.tile([P, H], U32, name=f"w_dealt{m}", align_bytes=64)
            nc.scalar.copy(out=dealt[:].rearrange("p (t c) -> p c t", t=PACK), in_=w_raw[m][:].rearrange("p (c t) -> p c t", t=PACK))
            w_dealt.append(dealt)
        ws_dealt = []
        for t in range(TILES):
            dealt = keep.tile([P, 2, P], U8, name=f"ws_dealt{t}", align_bytes=64)
            nc.vector.tensor_copy(dealt[:], ws_plane[:].rearrange("p (m c t) -> p t m c", m=2, t=PACK)[:, t])
            ws_dealt.append(dealt)

        def project(t, c0, c1):
            acc = psum.tile([P, c1 - c0], F32, name=f"y_acc{t}_{c0}", tag="acc")
            for m in (1, 0):
                nc.tensor.matmul_mx(
                    out=acc[:],
                    lhsT=w_dealt[m][:, t * P : (t + 1) * P].bitcast(FP8X4),
                    lhsT_scale=ws_dealt[t][:, m, :],
                    rhs=xw_got[:, m * S + c0 : m * S + c1].bitcast(FP8X4),
                    rhs_scale=x_plane[:, m * S + c0 : m * S + c1],
                    start=(m == 1),
                    stop=(m == 0),
                )
            return acc

        y = [keep.tile([P, S], F32, name=f"y{t}") for t in range(TILES)]
        nc.vector.tensor_copy(y[0][:, :HALF], project(0, 0, HALF)[:])
        nc.scalar.activation(y[0][:, HALF:], project(0, HALF, S)[:], COPY)
        for t in range(1, TILES):
            nc.vector.tensor_copy(y[t][:], project(t, 0, S)[:])

        ds_win = keep.tile([P, G], U8, name="ds_win", tag="then_d_scales", align_bytes=64)
        load_scale_rows(nc.sync, ds_win, d_scales)
        dw_win = keep.tile([P, G], U32, name="dw_win", tag="then_d_words", align_bytes=64)
        nc.sync.dma_start(out=dw_win[:].bitcast(I32), in_=words_of(d_words))
        l_k1 = load_list("l_k1", k1)
        l_n3 = load_list("l_n3", n3)
        l_n4 = load_list("l_n4", n4)
        l_n5 = load_list("l_n5", n5)
        gain = keep.tile([P, PACK], F32, name="gain")
        nc.gpsimd.dma_start(out=gain[:], in_=gs.rearrange("(p t) o -> p (t o)", t=PACK))
        ds_got = keep.tile([P, H], U8, name="ds_got", align_bytes=64)
        dw_got = keep.tile([P, H], U32, name="dw_got", align_bytes=64)

        def gather_codes(got, window, piece):
            nc.vector.tensor_copy(got[:, piece * 256 : (piece + 1) * 256], window[:].indirect(l_k1[:, piece * 16 : (piece + 1) * 16]))

        z_bf = keep.tile([P, S, PACK], BF16, name="z_bf", align_bytes=64)
        dt = [keep.tile([P, S + SPARE], F32, name=f"dt{t}") for t in range(TILES)]
        for t in range(TILES):
            nc.vector.memset(dt[t][:, S:], 0.0)

        rb = []
        for t in range(TILES):
            pa = keep.tile([P, W], F32, name=f"pa{t}")
            pb = keep.tile([P, W], F32, name=f"pb{t}")
            nc.scalar.activation(pb[:], y[t][:].indirect(l_n2[:]), COPY)
            nc.scalar.activation(pa[:], y[t][:].indirect(l_n1[:]), COPY)
            if t == TILES - 1:
                for piece in range(2):
                    gather_codes(ds_got, ds_win, piece)
                place_scale_rows((nc.sync,), d_plane, ds_got)
            diff = keep.tile([P, W], F32, name=f"rb{t}", tag="then_d_scales" if t == TILES - 1 else f"rb{t}", align_bytes=64)
            nc.vector.tensor_tensor(diff[:], pa[:], pb[:], SUB)
            rb.append(diff)
            nc.scalar.activation(dt[t][:].indirect(l_n1[:]), pb[:], COPY)
        for piece in range(2):
            gather_codes(dw_got, dw_win, piece)

        top = keep.tile([P, TILES, S], F32, name="top", tag="then_d_words", align_bytes=64)

        def larger(t, c0, c1):
            far = keep.tile([P, c1 - c0], F32, name=f"far{t}_{c0}")
            nc.scalar.activation(far[:], dt[t][:].indirect(l_n3[:, c0 // 16 : c1 // 16]), COPY)
            nc.vector.scalar_tensor_tensor(top[:, t, c0:c1], far[:], 0.5, dt[t][:, c0:c1], MULT, MAX)

        def weigh(t, c0, c1):
            nc.vector.tensor_scalar(z_bf[:, c0:c1, t], top[:, t, c0:c1], gain[:, t : t + 1], None, MULT)

        def put_differences(t):
            nc.scalar.activation(dt[t][:].indirect(l_n2[:]), rb[t][:], COPY)

        put_differences(0)
        for t in range(TILES - 1):
            if t + 1 < TILES - 1:
                put_differences(t + 1)
            larger(t, 0, S)
            weigh(t, 0, S)
        put_differences(TILES - 1)

        z_words = keep.tile([P, S], U32, name="z_words", align_bytes=64)
        z_plane = keep.tile([P, S], U8, name="z_plane", align_bytes=64)
        halves = [(a * HALF, (a + 1) * HALF) for a in range(2)]
        for c0, c1 in halves:
            larger(TILES - 1, c0, c1)
        for c0, c1 in halves:
            weigh(TILES - 1, c0, c1)
        for c0, c1 in halves:
            nc.vector.quantize_mx(out=z_words[:, c0:c1].bitcast(FP8X4), scales=z_plane[:, c0:c1], in_=z_bf[:, c0:c1, :].rearrange("p c t -> p (c t)"))

        def decode(t, c0, c1):
            acc = psum.tile([P, c1 - c0], F32, name=f"h_acc{t}_{c0}", tag="acc")
            nc.tensor.matmul_mx(
                out=acc[:],
                lhsT=dw_got[:, t * P : (t + 1) * P].bitcast(FP8X4),
                lhsT_scale=d_plane[:, t * P : (t + 1) * P],
                rhs=z_words[:, c0:c1].bitcast(FP8X4),
                rhs_scale=z_plane[:, c0:c1],
                start=True,
                stop=True,
            )
            return acc

        h = [keep.tile([P, S], F32, name=f"h{t}") for t in range(TILES)]
        for c0, c1 in halves:
            nc.scalar.activation(h[0][:, c0:c1], decode(0, c0, c1)[:], COPY, scale=0.0625)
        for t in range(1, TILES):
            nc.vector.tensor_scalar(h[t][:], decode(t, 0, S)[:], 0.0625, None, MULT)

        ra = []

        def put_back(t):
            nc.scalar.activation(h[t][:].indirect(l_n4[:]), ra[t][:], COPY)
            nc.sync.dma_start(out=out[t * P : (t + 1) * P, :], in_=h[t][:])

        for t in range(TILES):
            old = keep.tile([P, U], F32, name=f"old{t}")
            pa2 = keep.tile([P, U], F32, name=f"pa2_{t}")
            new = keep.tile([P, U], F32, name=f"ra{t}")
            nc.scalar.activation(old[:], h[t][:].indirect(l_n4[:]), COPY)
            nc.scalar.activation(pa2[:], h[t][:].indirect(l_n5[:]), COPY)
            nc.vector.scalar_tensor_tensor(new[:], pa2[:], -0.5, old[:], MULT, ADD)
            ra.append(new)
            if t > 0:
                put_back(t - 1)
        put_back(TILES - 1)
